import numpy as np
import ml_dtypes


def mxq(x, axis, fmt="e4m3"):
    dtype, down = {"e4m3": (ml_dtypes.float8_e4m3fn, 7), "e5m2": (ml_dtypes.float8_e5m2, 14)}[fmt]
    v = np.moveaxis(np.asarray(x, np.float32).astype(ml_dtypes.bfloat16).astype(np.float64), axis, -1)
    blocks = v.reshape(v.shape[:-1] + (-1, 32))
    amax = np.abs(blocks).max(-1, keepdims=True)
    byte = np.maximum(np.where(amax > 0, np.frexp(amax)[1] - 1 + 127, 0) - down, 1)
    scale = np.exp2(byte - 127.0)
    codes = (blocks / scale).astype(np.float32).astype(dtype).astype(np.float64)
    return np.moveaxis((codes * scale).reshape(v.shape), -1, axis)


WIDE = False


def mx_kscale(k):
    if not WIDE:
        return np.ones(k)
    levels = np.array([10, -10, 5, -5, 0])
    if k % 512:
        return np.exp2(np.random.permutation(np.resize(levels, k // 32))).repeat(32)
    a = np.empty((k // 512, 16))
    for p in range(k // 512):
        a[p, :8] = np.random.permutation(np.resize(levels, 8))
        for g in range(8):
            far = levels[np.abs(levels - a[p, g]) >= 10]
            a[p, g + 8] = far[np.random.randint(len(far))]
    return np.exp2(a.ravel()).repeat(32)


BF16 = ml_dtypes.bfloat16


def bf(x):
    return np.asarray(x, np.float32).astype(BF16)


def f64(x):
    return np.asarray(x).astype(np.float64)


T, D, C, E, F = 1024, 512, 512, 4, 512

TEMPERATURE = 0.05


def draw0():
    s, t = mx_kscale(D), mx_kscale(C)
    s = s / np.exp2(np.round(np.log2(np.sqrt(np.mean(s * s)))))
    return {"x": bf(np.random.standard_normal((T, D)) * s),
            "enc": bf(np.random.standard_normal((E, D, C)) / np.sqrt(D) / s[:, None]),
            "c": bf((1.0 + 0.2 * np.random.standard_normal((E, C))) * t),
            "dec": bf(np.random.standard_normal((E, C, D)) / np.sqrt(C) / t[:, None]),
            "w": bf(np.random.standard_normal((E, D, F)) / np.sqrt(D) / s[:, None])}


def core(x, enc, c, dec, w):
    xf = f64(x)
    xq = mxq(xf, 1, "e4m3")
    p = xq @ mxq(f64(enc), 1, "e4m3")
    code = np.tanh(p) * f64(c)[:, None, :]
    rec = mxq(code, 2, "e4m3") @ mxq(f64(dec), 1, "e4m3")
    err = np.mean(np.square(xf[None, :, :] - rec), axis=-1)
    z = -err / TEMPERATURE
    ez = np.exp(z - z.max(axis=0, keepdims=True))
    g = ez / ez.sum(axis=0, keepdims=True)
    q = xq @ mxq(f64(w), 1, "e4m3")
    return np.sum(g[:, :, None] * q, axis=0)


def e4m3fn_bytes(y):
    return np.clip(np.asarray(y, np.float64), -448.0, 448.0).astype(np.float32).astype(ml_dtypes.float8_e4m3fn).view(np.uint8)


def e4m3fn_values(b):
    return np.asarray(b, np.uint8).view(ml_dtypes.float8_e4m3fn).astype(np.float64)


def setup_inputs():
    d = draw0()
    x0 = np.asarray(d['w']).astype(np.float64)
    s = (np.max(np.abs(x0), axis=(0, 2), keepdims=True) / 448.0).astype(np.float32)
    out = {}
    for k, v in d.items():
        if k == 'w':
            out['w_bytes'] = e4m3fn_bytes(x0 / s.astype(np.float64))
            out['w_scale'] = s
        else:
            out[k] = v
    return out


def reference(x, enc, c, dec, w_bytes, w_scale):
    return core(x, enc, c, dec, e4m3fn_values(w_bytes) * w_scale.astype(np.float64))

@@ -1,0 +1,373 @@
+import math
+from contextlib import ExitStack
+
+import concourse.mybir as mybir
+from concourse.masks import make_identity
+
+T, D, C, E, F = 1024, 512, 512, 4, 512
+TEMPERATURE = 0.05
+FLOPS = 3 * E * 2 * T * D * C
+
+F32 = mybir.dt.float32
+BF16 = mybir.dt.bfloat16
+U32 = mybir.dt.uint32
+U8 = mybir.dt.uint8
+FP8 = mybir.dt.float8_e4m3fn
+FP8X4 = mybir.dt.float8_e4m3fn_x4
+ACT = mybir.ActivationFunctionType
+ALU = mybir.AluOpType
+
+P = 128
+PACK = 4
+TILES = T // P
+PAIRS = TILES // 2
+HALF_TILES = TILES // 2
+STEPS = 2 * E
+W_HALF = F // 2
+ERR_SCALE = math.sqrt(1.0 / (D * TEMPERATURE))
+
+
+def tile_expertgateautoencoderrouting_kernel(tc, x, enc, c, dec, w_bytes, w_scale, out):
+    nc = tc.nc
+    with ExitStack() as ctx:
+        keep = ctx.enter_context(tc.tile_pool(name="keep", bufs=1))
+        work = ctx.enter_context(tc.tile_pool(name="work", bufs=1))
+        psum = ctx.enter_context(tc.psum_pool(name="psum", bufs=8))
+        ctx.enter_context(tc.manual_schedule())
+
+        def bank(shape, name):
+            return psum.tile(shape, F32, name=name, tag="bank")
+
+        def mx_pair(name, width):
+            codes = keep.tile([P, width], U32, name=name + "_codes", align_bytes=64)
+            scales = keep.tile([P, width], U8, name=name + "_scales", align_bytes=64)
+            return codes, scales
+
+        def quantize(pair, cols, src):
+            nc.vector.quantize_mx(out=pair[0][:, cols].bitcast(FP8X4), scales=pair[1][:, cols], in_=src)
+
+        def mx_matmul(dst, lhs, lhs_cols, rhs, rhs_cols):
+            nc.tensor.matmul_mx(
+                out=dst,
+                lhsT=lhs[0][:, lhs_cols].bitcast(FP8X4),
+                lhsT_scale=lhs[1][:, lhs_cols],
+                rhs=rhs[0][:, rhs_cols].bitcast(FP8X4),
+                rhs_scale=rhs[1][:, rhs_cols],
+                start=True,
+                stop=True,
+            )
+
+        c_bf = keep.tile([P, E, PACK], BF16, name="c_bf")
+        nc.scalar.dma_start(out=c_bf[:], in_=c.rearrange("e (p t) -> p e t", t=PACK))
+        ws = keep.tile([P, PACK], F32, name="ws")
+        nc.scalar.dma_start(out=ws[:], in_=w_scale.rearrange("o (p t) z -> p (o t z)", t=PACK))
+
+        def load_rows(name, src, dtype):
+            raw = keep.tile([P, PACK, 512], dtype, name=name, align_bytes=256)
+            nc.sync.dma_start(out=raw[:], in_=src.rearrange("(p j) n -> p j n", j=PACK))
+            return raw
+
+        x_rows = x.rearrange("(q p n) d -> q p n d", p=P, n=2)
+        out_rows = out.rearrange("(q p n) f -> q n p f", p=P, n=2)
+        enc_raw, dec_raw, w_raw, x_sb = {}, {}, {}, {}
+        enc_raw[0] = load_rows("enc_raw0", enc[0], BF16)
+        for q in range(PAIRS):
+            x_sb[q] = keep.tile([P, 2, D], BF16, name="x_sb%d" % q, align_bytes=256)
+            nc.sync.dma_start(out=x_sb[q][:], in_=x_rows[q])
+        dec_raw[0] = load_rows("dec_raw0", dec[0], BF16)
+        for e in range(E):
+            if e + 1 < E:
+                enc_raw[e + 1] = load_rows("enc_raw%d" % (e + 1), enc[e + 1], BF16)
+            w_raw[e] = load_rows("w_raw%d" % e, w_bytes[e], U8)
+            if e + 1 < E:
+                dec_raw[e + 1] = load_rows("dec_raw%d" % (e + 1), dec[e + 1], BF16)
+
+        ident = keep.tile([P, P], F32, name="ident")
+        make_identity(nc, ident[:])
+
+        xq = mx_pair("x", T)
+        encq = [mx_pair("enc%d" % e, C) for e in range(E)]
+        decq = [mx_pair("dec%d" % e, D) for e in range(E)]
+        wq = [mx_pair("w%d" % e, F) for e in range(E)]
+        ssq = keep.tile([P, TILES, E], F32, name="ssq")
+
+        c_f32 = keep.tile([P, E * PACK], F32, name="c_f32")
+        nc.scalar.activation(out=c_f32[:], in_=c_bf[:].rearrange("p e t -> p (e t)"), func=ACT.Copy)
+        gain = bank([P, E * PACK], "gain")
+        nc.tensor.matmul(gain[:], lhsT=ident[:], rhs=c_f32[:], start=True, stop=True)
+
+        def enc_views(stage, raw):
+            return (
+                stage[:].rearrange("p (t m j) -> p t m j", t=PACK, j=PACK),
+                raw[:].rearrange("p j (m t) -> p t m j", t=PACK),
+            )
+
+        def plain_views(stage, raw):
+            return stage[:].rearrange("p (n j) -> p n j", j=PACK), raw[:].rearrange("p j n -> p n j")
+
+        def stage_tile(tag, width):
+            return work.tile([P, width], BF16, name=tag, tag=tag, align_bytes=64)
+
+        def interleave_gpsimd(views):
+            nc.gpsimd.tensor_scalar(views[0], views[1], 1.0, 0.0, op0=ALU.mult, op1=ALU.add)
+
+        planes = {}
+
+        def widen_w(k, slots):
+            e, h = divmod(k, 2)
+            if k not in planes:
+                planes[k] = work.tile([P, PACK, W_HALF], BF16, name="w_planes", tag="w_planes", bufs=3)
+            for t in slots:
+                nc.scalar.activation(
+                    out=planes[k][:, t, :],
+                    in_=w_raw[e][:, t, h * W_HALF : (h + 1) * W_HALF].bitcast(FP8),
+                    func=ACT.Copy,
+                    scale=ws[:, t : t + 1],
+                )
+
+        x_grouped = {}
+
+        def turn_x(q):
+            words = x_sb[q][:].rearrange("p n d -> p (n d)").bitcast(F32)
+            xt = bank([P, 2, 2, P], "xt")
+            for n in range(2):
+                for u in range(2):
+                    nc.tensor.transpose(xt[:, n, u, :], words[:, 256 * n + u : 256 * (n + 1) : 2], ident[:])
+            x_grouped[q] = stage_tile("stage_first" if q == PAIRS - 1 else "x_grouped%d" % q, 2 * P * PACK)
+            nc.scalar.copy(
+                out=x_grouped[q][:].bitcast(F32).rearrange("p (n r u) -> p n r u", n=2, u=2),
+                in_=xt[:].rearrange("p n u r -> p n r u"),
+            )
+
+        def quantize_x(q):
+            quantize(xq, slice(2 * P * q, 2 * P * (q + 1)), x_grouped[q][:])
+
+        p_banks, tanh_sb, code_bf, codeq, rec_banks, diffs = {}, {}, {}, {}, {}, {}
+
+        def encode(u):
+            e, q = divmod(u, PAIRS)
+            for n in range(2):
+                j = 2 * q + n
+                p_banks[u, n] = bank([P, PACK, P], "p_bank")
+                for t in range(PACK):
+                    mx_matmul(p_banks[u, n][:, t, :], encq[e], slice(P * t, P * (t + 1)), xq, slice(P * j, P * (j + 1)))
+
+        def tanh(u):
+            tanh_sb[u] = work.tile([P, 2, P, PACK], F32, name="tanh_sb", tag="tanh_sb", bufs=3)
+            for n in range(2):
+                nc.scalar.activation(
+                    out=tanh_sb[u][:, n, :, :], in_=p_banks[u, n][:].rearrange("p t r -> p r t"), func=ACT.Tanh
+                )
+
+        def apply_gain(u):
+            e = u // PAIRS
+            s, i = divmod(u, 2)
+            if i == 0:
+                code_bf[s] = work.tile([P, 2, 2 * P, PACK], BF16, name="code_bf", tag="code_bf", bufs=2, align_bytes=64)
+            nc.vector.tensor_tensor(
+                out=code_bf[s][:, i, :, :],
+                in0=tanh_sb[u][:].rearrange("p n r t -> p (n r) t"),
+                in1=gain[:, PACK * e : PACK * (e + 1)].unsqueeze(1).to_broadcast([P, 2 * P, PACK]),
+                op=ALU.mult,
+            )
+
+        def quantize_code(s):
+            codes = work.tile([P, 4 * P], U32, name="code_codes", tag="code_codes", bufs=2, align_bytes=64)
+            scales = work.tile([P, 4 * P], U8, name="code_scales", tag="code_scales", bufs=2, align_bytes=64)
+            codeq[s] = (codes, scales)
+            quantize(codeq[s], slice(0, 4 * P), code_bf[s][:].rearrange("p i r t -> p (i r t)"))
+
+        def decode(s):
+            for i in range(HALF_TILES):
+                rec_banks[s, i] = bank([P, D], "rec_bank")
+                mx_matmul(rec_banks[s, i][:], codeq[s], slice(P * i, P * (i + 1)), decq[s // 2], slice(0, D))
+
+        def subtract(s, i):
+            j = HALF_TILES * (s % 2) + i
+            diffs[s, i] = work.tile([P, D], F32, name="diff", tag="diff", bufs=4)
+            nc.vector.tensor_tensor(
+                out=diffs[s, i][:], in0=rec_banks[s, i][:], in1=x_sb[j // 2][:, j % 2, :], op=ALU.subtract
+            )
+
+        def square_sum(s, i):
+            j = HALF_TILES * (s % 2) + i
+            e = s // 2
+            nc.scalar.activation(
+                out=diffs[s, i][:], in_=diffs[s, i][:], func=ACT.Square, scale=ERR_SCALE, accum_out=ssq[:, j, e : e + 1]
+            )
+
+        stage = stage_tile("head_enc", 2048)
+        views = enc_views(stage, enc_raw[0])
+        nc.vector.tensor_copy(out=views[0], in_=views[1])
+        turn_x(0)
+        quantize(encq[0], slice(0, C), stage[:])
+        turn_x(1)
+        quantize_x(0)
+        turn_x(2)
+        quantize_x(1)
+        turn_x(3)
+        quantize_x(2)
+        stage = stage_tile("head_dec", 2048)
+        views = plain_views(stage, dec_raw[0])
+        nc.vector.tensor_copy(out=views[0], in_=views[1])
+        quantize_x(3)
+        encode(0)
+        tanh(0)
+        encode(1)
+        head_dec = stage
+
+        def w_halves(s):
+            if s == 0:
+                return []
+            if s < STEPS - 2:
+                return [s - 1]
+            if s == STEPS - 2:
+                return [s - 1, s]
+            return [s]
+
+        units = 2 * STEPS
+        for s in range(STEPS):
+            jobs = []
+            if s < STEPS - 2:
+                e = s // 2 + 1
+                stage = stage_tile("stage_first", 2048)
+                if s % 2 == 0:
+                    interleave_gpsimd(enc_views(stage, enc_raw[e]))
+                    jobs.append((encq[e], slice(0, C), stage[:]))
+                else:
+                    interleave_gpsimd(plain_views(stage, dec_raw[e]))
+                    jobs.append((decq[e], slice(0, D), stage[:]))
+            for k in w_halves(s):
+                stage = stage_tile("stage_second" if jobs else "stage_first", PACK * W_HALF)
+                interleave_gpsimd(plain_views(stage, planes[k]))
+                jobs.append((wq[k // 2], slice(W_HALF * (k % 2), W_HALF * (k % 2 + 1)), stage[:]))
+
+            if s > 0:
+                decode(s - 1)
+            apply_gain(2 * s)
+            tanh(2 * s + 1)
+            if 2 * s + 2 < units:
+                encode(2 * s + 2)
+            if s == 0:
+                jobs.append((decq[0], slice(0, D), head_dec[:]))
+                widen_w(0, range(PACK))
+            if s + 1 < STEPS:
+                widen_w(s + 1, range(0, 2))
+            if s > 0:
+                for i in range(3):
+                    subtract(s - 1, i)
+                    square_sum(s - 1, i)
+            apply_gain(2 * s + 1)
+            if 2 * s + 2 < units:
+                tanh(2 * s + 2)
+                encode(2 * s + 3)
+            if s > 0:
+                subtract(s - 1, 3)
+                square_sum(s - 1, 3)
+            if s + 1 < STEPS:
+                widen_w(s + 1, range(2, PACK))
+            quantize_code(s)
+            for job in reversed(jobs):
+                quantize(*job)
+
+        least, ez, total, inv, gate = {}, {}, {}, {}, {}
+
+        def gate_min(h):
+            least[h] = keep.tile([P, HALF_TILES], F32, name="least%d" % h)
+            tiles = slice(HALF_TILES * h, HALF_TILES * (h + 1))
+            nc.vector.tensor_reduce(out=least[h][:], in_=ssq[:, tiles, :], axis=mybir.AxisListType.X, op=ALU.min)
+
+        def gate_exp(h):
+            ez[h] = keep.tile([P, HALF_TILES, E], F32, name="ez%d" % h)
+            total[h] = keep.tile([P, HALF_TILES], F32, name="total%d" % h)
+            for i in range(HALF_TILES):
+                nc.scalar.activation(
+                    out=ez[h][:, i, :],
+                    in_=ssq[:, HALF_TILES * h + i, :],
+                    func=ACT.Exp,
+                    scale=-1.0,
+                    bias=least[h][:, i : i + 1],
+                    accum_out=total[h][:, i : i + 1],
+                )
+
+        def gate_inverse(h):
+            inv[h] = keep.tile([P, HALF_TILES], F32, name="inv%d" % h)
+            nc.vector.reciprocal(out=inv[h][:], in_=total[h][:])
+
+        def gate_normalise(h):
+            gate[h] = keep.tile([P, HALF_TILES, E], F32, name="gate%d" % h)
+            for i in range(HALF_TILES):
+                nc.scalar.activation(out=gate[h][:, i, :], in_=ez[h][:, i, :], func=ACT.Copy, scale=inv[h][:, i : i + 1])
+
+        q_banks, terms = {}, {}
+
+        def project(j):
+            for e in (0, 2, 1, 3):
+                q_banks[j, e] = bank([P, F], "q_bank")
+                mx_matmul(q_banks[j, e][:], xq, slice(P * j, P * (j + 1)), wq[e], slice(0, F))
+
+        def g_col(j, e):
+            return gate[j // HALF_TILES][:, j % HALF_TILES, e : e + 1]
+
+        def scalar_experts(j):
+            return (0,) if j == TILES - 1 else (0, 2)
+
+        def scalar_terms(j):
+            for e in scalar_experts(j):
+                terms[j, e] = work.tile([P, F], F32, name="term", tag="term", bufs=4)
+                nc.scalar.activation(out=terms[j, e][:], in_=q_banks[j, e][:], func=ACT.Copy, scale=g_col(j, e))
+
+        def add_term(j, e, acc):
+            res = work.tile([P, F], F32, name="partial", tag="partial", bufs=6)
+            nc.vector.scalar_tensor_tensor(
+                out=res[:], in0=q_banks[j, e][:], scalar=g_col(j, e), in1=acc[:], op0=ALU.mult, op1=ALU.add
+            )
+            return res
+
+        def finish(j):
+            if len(scalar_experts(j)) == 2:
+                low = add_term(j, 1, terms[j, 0])
+                high = add_term(j, 3, terms[j, 2])
+                res = work.tile([P, F], F32, name="result", tag="result", bufs=3)
+                nc.gpsimd.tensor_tensor(out=res[:], in0=low[:], in1=high[:], op=ALU.add)
+            else:
+                res = terms[j, 0]
+                for e in (2, 1, 3):
+                    res = add_term(j, e, res)
+            nc.sync.dma_start(out=out_rows[j // 2, j % 2], in_=res[:])
+
+        last = STEPS - 1
+        decode(last)
+        gate_min(0)
+        gate_exp(0)
+        project(0)
+        subtract(last, 0)
+        gate_inverse(0)
+        gate_normalise(0)
+        for i in range(1, HALF_TILES):
+            subtract(last, i)
+        project(1)
+        scalar_terms(0)
+        square_sum(last, 0)
+        square_sum(last, 1)
+        finish(0)
+        project(2)
+        scalar_terms(1)
+        square_sum(last, 2)
+        square_sum(last, 3)
+        finish(1)
+        project(3)
+        scalar_terms(2)
+        gate_min(1)
+        gate_exp(1)
+        finish(2)
+        project(4)
+        scalar_terms(3)
+        gate_inverse(1)
+        gate_normalise(1)
+        finish(3)
+        for j in range(HALF_TILES, TILES):
+            if j + 1 < TILES:
+                project(j + 1)
+            scalar_terms(j)
+            finish(j)

@@ -23,7 +23,10 @@ TILES = T // P
 PAIRS = TILES // 2
 HALF_TILES = TILES // 2
 STEPS = 2 * E
-W_HALF = F // 2
+W_CUTS = (0, 176, 344, F)
+DEC_AFTER = 1
+HEAD_PLANES = 6
+VECTOR_ONLY = (6, 7)
 ERR_SCALE = math.sqrt(1.0 / (D * TEMPERATURE))
 
 
@@ -74,7 +77,8 @@ def tile_expertgateautoencoderrouting_kernel(tc, x, enc, c, dec, w_bytes, w_scal
         for q in range(PAIRS):
             x_sb[q] = keep.tile([P, 2, D], BF16, name="x_sb%d" % q, align_bytes=256)
             nc.sync.dma_start(out=x_sb[q][:], in_=x_rows[q])
-        dec_raw[0] = load_rows("dec_raw0", dec[0], BF16)
+            if q == DEC_AFTER:
+                dec_raw[0] = load_rows("dec_raw0", dec[0], BF16)
         for e in range(E):
             if e + 1 < E:
                 enc_raw[e + 1] = load_rows("enc_raw%d" % (e + 1), enc[e + 1], BF16)
@@ -113,61 +117,63 @@ def tile_expertgateautoencoderrouting_kernel(tc, x, enc, c, dec, w_bytes, w_scal
 
         planes = {}
 
-        def widen_w(k, slots):
-            e, h = divmod(k, 2)
-            if k not in planes:
-                planes[k] = work.tile([P, PACK, W_HALF], BF16, name="w_planes", tag="w_planes", bufs=3)
+        def widen_w(e, slots):
+            if e not in planes:
+                planes[e] = work.tile([P, PACK, F], BF16, name="w_planes", tag="w_planes", bufs=4)
             for t in slots:
                 nc.scalar.activation(
-                    out=planes[k][:, t, :],
-                    in_=w_raw[e][:, t, h * W_HALF : (h + 1) * W_HALF].bitcast(FP8),
-                    func=ACT.Copy,
-                    scale=ws[:, t : t + 1],
+                    out=planes[e][:, t, :], in_=w_raw[e][:, t, :].bitcast(FP8), func=ACT.Copy, scale=ws[:, t : t + 1]
                 )
 
         x_grouped = {}
 
-        def turn_x(q):
-            words = x_sb[q][:].rearrange("p n d -> p (n d)").bitcast(F32)
-            xt = bank([P, 2, 2, P], "xt")
-            for n in range(2):
+        def turn_x(first, count, engine_copy, tag):
+            xt = bank([P, count, 2, P], "xt")
+            for i in range(count):
+                q, n = divmod(first + i, 2)
+                words = x_sb[q][:].rearrange("p n d -> p (n d)").bitcast(F32)
                 for u in range(2):
-                    nc.tensor.transpose(xt[:, n, u, :], words[:, 256 * n + u : 256 * (n + 1) : 2], ident[:])
-            x_grouped[q] = stage_tile("stage_first" if q == PAIRS - 1 else "x_grouped%d" % q, 2 * P * PACK)
-            nc.scalar.copy(
-                out=x_grouped[q][:].bitcast(F32).rearrange("p (n r u) -> p n r u", n=2, u=2),
-                in_=xt[:].rearrange("p n u r -> p n r u"),
-            )
+                    nc.tensor.transpose(xt[:, i, u, :], words[:, 256 * n + u : 256 * (n + 1) : 2], ident[:])
+            x_grouped[first] = stage_tile(tag, count * P * PACK)
 
-        def quantize_x(q):
-            quantize(xq, slice(2 * P * q, 2 * P * (q + 1)), x_grouped[q][:])
+            def empty():
+                engine_copy(
+                    out=x_grouped[first][:].bitcast(F32).rearrange("p (n r u) -> p n r u", n=count, u=2),
+                    in_=xt[:].rearrange("p n u r -> p n r u"),
+                )
+
+            return empty
+
+        def quantize_x(first, count):
+            quantize(xq, slice(P * first, P * (first + count)), x_grouped[first][:])
 
         p_banks, tanh_sb, code_bf, codeq, rec_banks, diffs = {}, {}, {}, {}, {}, {}
 
-        def encode(u):
-            e, q = divmod(u, PAIRS)
-            for n in range(2):
-                j = 2 * q + n
-                p_banks[u, n] = bank([P, PACK, P], "p_bank")
+        def encode(s, tiles):
+            for i in tiles:
+                j = HALF_TILES * (s % 2) + i
+                p_banks[s, i] = bank([P, PACK, P], "p_bank")
                 for t in range(PACK):
-                    mx_matmul(p_banks[u, n][:, t, :], encq[e], slice(P * t, P * (t + 1)), xq, slice(P * j, P * (j + 1)))
+                    mx_matmul(
+                        p_banks[s, i][:, t, :], encq[s // 2], slice(P * t, P * (t + 1)), xq, slice(P * j, P * (j + 1))
+                    )
 
-        def tanh(u):
-            tanh_sb[u] = work.tile([P, 2, P, PACK], F32, name="tanh_sb", tag="tanh_sb", bufs=3)
-            for n in range(2):
+        def tanh(s, tiles):
+            if s not in tanh_sb:
+                tanh_sb[s] = work.tile([P, HALF_TILES, P, PACK], F32, name="tanh_sb", tag="tanh_sb", bufs=2)
+            for i in tiles:
                 nc.scalar.activation(
-                    out=tanh_sb[u][:, n, :, :], in_=p_banks[u, n][:].rearrange("p t r -> p r t"), func=ACT.Tanh
+                    out=tanh_sb[s][:, i, :, :], in_=p_banks[s, i][:].rearrange("p t r -> p r t"), func=ACT.Tanh
                 )
 
-        def apply_gain(u):
-            e = u // PAIRS
-            s, i = divmod(u, 2)
-            if i == 0:
-                code_bf[s] = work.tile([P, 2, 2 * P, PACK], BF16, name="code_bf", tag="code_bf", bufs=2, align_bytes=64)
+        def apply_gain(s, first, last):
+            e = s // 2
+            if first == 0:
+                code_bf[s] = work.tile([P, HALF_TILES * P, PACK], BF16, name="code_bf", tag="code_bf", bufs=2, align_bytes=64)
             nc.vector.tensor_tensor(
-                out=code_bf[s][:, i, :, :],
-                in0=tanh_sb[u][:].rearrange("p n r t -> p (n r) t"),
-                in1=gain[:, PACK * e : PACK * (e + 1)].unsqueeze(1).to_broadcast([P, 2 * P, PACK]),
+                out=code_bf[s][:, P * first : P * last, :],
+                in0=tanh_sb[s][:, first:last, :, :].rearrange("p n r t -> p (n r) t"),
+                in1=gain[:, PACK * e : PACK * (e + 1)].unsqueeze(1).to_broadcast([P, P * (last - first), PACK]),
                 op=ALU.mult,
             )
 
@@ -175,10 +181,10 @@ def tile_expertgateautoencoderrouting_kernel(tc, x, enc, c, dec, w_bytes, w_scal
             codes = work.tile([P, 4 * P], U32, name="code_codes", tag="code_codes", bufs=2, align_bytes=64)
             scales = work.tile([P, 4 * P], U8, name="code_scales", tag="code_scales", bufs=2, align_bytes=64)
             codeq[s] = (codes, scales)
-            quantize(codeq[s], slice(0, 4 * P), code_bf[s][:].rearrange("p i r t -> p (i r t)"))
+            quantize(codeq[s], slice(0, 4 * P), code_bf[s][:].rearrange("p r t -> p (r t)"))
 
-        def decode(s):
-            for i in range(HALF_TILES):
+        def decode(s, tiles):
+            for i in tiles:
                 rec_banks[s, i] = bank([P, D], "rec_bank")
                 mx_matmul(rec_banks[s, i][:], codeq[s], slice(P * i, P * (i + 1)), decq[s // 2], slice(0, D))
 
@@ -195,80 +201,6 @@ def tile_expertgateautoencoderrouting_kernel(tc, x, enc, c, dec, w_bytes, w_scal
             nc.scalar.activation(
                 out=diffs[s, i][:], in_=diffs[s, i][:], func=ACT.Square, scale=ERR_SCALE, accum_out=ssq[:, j, e : e + 1]
             )
-
-        stage = stage_tile("head_enc", 2048)
-        views = enc_views(stage, enc_raw[0])
-        nc.vector.tensor_copy(out=views[0], in_=views[1])
-        turn_x(0)
-        quantize(encq[0], slice(0, C), stage[:])
-        turn_x(1)
-        quantize_x(0)
-        turn_x(2)
-        quantize_x(1)
-        turn_x(3)
-        quantize_x(2)
-        stage = stage_tile("head_dec", 2048)
-        views = plain_views(stage, dec_raw[0])
-        nc.vector.tensor_copy(out=views[0], in_=views[1])
-        quantize_x(3)
-        encode(0)
-        tanh(0)
-        encode(1)
-        head_dec = stage
-
-        def w_halves(s):
-            if s == 0:
-                return []
-            if s < STEPS - 2:
-                return [s - 1]
-            if s == STEPS - 2:
-                return [s - 1, s]
-            return [s]
-
-        units = 2 * STEPS
-        for s in range(STEPS):
-            jobs = []
-            if s < STEPS - 2:
-                e = s // 2 + 1
-                stage = stage_tile("stage_first", 2048)
-                if s % 2 == 0:
-                    interleave_gpsimd(enc_views(stage, enc_raw[e]))
-                    jobs.append((encq[e], slice(0, C), stage[:]))
-                else:
-                    interleave_gpsimd(plain_views(stage, dec_raw[e]))
-                    jobs.append((decq[e], slice(0, D), stage[:]))
-            for k in w_halves(s):
-                stage = stage_tile("stage_second" if jobs else "stage_first", PACK * W_HALF)
-                interleave_gpsimd(plain_views(stage, planes[k]))
-                jobs.append((wq[k // 2], slice(W_HALF * (k % 2), W_HALF * (k % 2 + 1)), stage[:]))
-
-            if s > 0:
-                decode(s - 1)
-            apply_gain(2 * s)
-            tanh(2 * s + 1)
-            if 2 * s + 2 < units:
-                encode(2 * s + 2)
-            if s == 0:
-                jobs.append((decq[0], slice(0, D), head_dec[:]))
-                widen_w(0, range(PACK))
-            if s + 1 < STEPS:
-                widen_w(s + 1, range(0, 2))
-            if s > 0:
-                for i in range(3):
-                    subtract(s - 1, i)
-                    square_sum(s - 1, i)
-            apply_gain(2 * s + 1)
-            if 2 * s + 2 < units:
-                tanh(2 * s + 2)
-                encode(2 * s + 3)
-            if s > 0:
-                subtract(s - 1, 3)
-                square_sum(s - 1, 3)
-            if s + 1 < STEPS:
-                widen_w(s + 1, range(2, PACK))
-            quantize_code(s)
-            for job in reversed(jobs):
-                quantize(*job)
 
         least, ez, total, inv, gate = {}, {}, {}, {}, {}
 
@@ -301,8 +233,8 @@ def tile_expertgateautoencoderrouting_kernel(tc, x, enc, c, dec, w_bytes, w_scal
 
         q_banks, terms = {}, {}
 
-        def project(j):
-            for e in (0, 2, 1, 3):
+        def project(j, experts=(0, 2, 1, 3)):
+            for e in experts:
                 q_banks[j, e] = bank([P, F], "q_bank")
                 mx_matmul(q_banks[j, e][:], xq, slice(P * j, P * (j + 1)), wq[e], slice(0, F))
 
@@ -310,46 +242,172 @@ def tile_expertgateautoencoderrouting_kernel(tc, x, enc, c, dec, w_bytes, w_scal
             return gate[j // HALF_TILES][:, j % HALF_TILES, e : e + 1]
 
         def scalar_experts(j):
-            return (0,) if j == TILES - 1 else (0, 2)
+            return (0,) if j in VECTOR_ONLY else (0, 2)
 
         def scalar_terms(j):
             for e in scalar_experts(j):
-                terms[j, e] = work.tile([P, F], F32, name="term", tag="term", bufs=4)
+                terms[j, e] = work.tile([P, F], F32, name="term", tag="term", bufs=6)
                 nc.scalar.activation(out=terms[j, e][:], in_=q_banks[j, e][:], func=ACT.Copy, scale=g_col(j, e))
 
         def add_term(j, e, acc):
-            res = work.tile([P, F], F32, name="partial", tag="partial", bufs=6)
+            res = work.tile([P, F], F32, name="partial", tag="partial", bufs=10)
             nc.vector.scalar_tensor_tensor(
                 out=res[:], in0=q_banks[j, e][:], scalar=g_col(j, e), in1=acc[:], op0=ALU.mult, op1=ALU.add
             )
             return res
 
+        sums = {}
+
+        def vector_steps(j):
+            def pair_step(e):
+                def step():
+                    sums[j, e] = add_term(j, e, terms[j, e - 1])
+                    if e == 3:
+                        res = work.tile([P, F], F32, name="result", tag="result", bufs=3)
+                        nc.gpsimd.tensor_tensor(out=res[:], in0=sums[j, 1][:], in1=sums[j, 3][:], op=ALU.add)
+                        nc.sync.dma_start(out=out_rows[j // 2, j % 2], in_=res[:])
+
+                return step
+
+            def chain_step(e, before):
+                def step():
+                    sums[j, e] = add_term(j, e, terms[j, 0] if before is None else sums[j, before])
+                    if e == 3:
+                        nc.sync.dma_start(out=out_rows[j // 2, j % 2], in_=sums[j, e][:])
+
+                return step
+
+            if j in VECTOR_ONLY:
+                return [chain_step(2, None), chain_step(1, 2), chain_step(3, 1)]
+            return [pair_step(1), pair_step(3)]
+
         def finish(j):
-            if len(scalar_experts(j)) == 2:
-                low = add_term(j, 1, terms[j, 0])
-                high = add_term(j, 3, terms[j, 2])
-                res = work.tile([P, F], F32, name="result", tag="result", bufs=3)
-                nc.gpsimd.tensor_tensor(out=res[:], in0=low[:], in1=high[:], op=ALU.add)
+            for step in vector_steps(j):
+                step()
+
+        head_enc = stage_tile("head_enc", 2048)
+        views = enc_views(head_enc, enc_raw[0])
+        nc.vector.tensor_copy(out=views[0], in_=views[1])
+        turn_x(0, 1, nc.scalar.copy, "x_grouped0")()
+        turn_x(1, 1, nc.scalar.copy, "x_grouped1")()
+        quantize(encq[0], slice(0, C), head_enc[:])
+        quantize_x(0, 1)
+        quantize_x(1, 1)
+        turn_x(2, 2, nc.scalar.copy, "x_grouped2")()
+        encode(0, (0, 1))
+        head_dec = stage_tile("stage_first", 2048)
+        views = plain_views(head_dec, dec_raw[0])
+        nc.vector.tensor_copy(out=views[0], in_=views[1])
+        tanh(0, (0, 1))
+        quantize_x(2, 2)
+        quantize(decq[0], slice(0, D), head_dec[:])
+        empty_third = turn_x(4, 2, nc.vector.tensor_copy, "x_grouped4")
+        encode(0, (2, 3))
+        empty_fourth = turn_x(6, 2, nc.vector.tensor_copy, "x_grouped6")
+
+        w_stage = {}
+
+        def interleave_w(e, piece):
+            if piece == 0:
+                w_stage[e] = stage_tile("stage_second", PACK * F)
+            cols = slice(W_CUTS[piece], W_CUTS[piece + 1])
+            views = plain_views(w_stage[e], planes[e])
+            interleave_gpsimd((views[0][:, cols, :], views[1][:, cols, :]))
+
+        to_widen = [(e, t) for e in range(E) for t in range(PACK)]
+
+        def widen_next():
+            if to_widen:
+                e, t = to_widen.pop(0)
+                widen_w(e, [t])
+
+        pieces = len(W_CUTS) - 1
+        for s in range(STEPS):
+            jobs = []
+            stage = stage_tile("stage_first", 2048)
+            if s >= STEPS - 2:
+                e = s - (STEPS - E)
+                interleave_gpsimd(plain_views(stage, planes[e]))
+                jobs.append((wq[e], slice(0, F), stage[:]))
+            elif s % 2 == 0:
+                e = s // 2 + 1
+                interleave_gpsimd(enc_views(stage, enc_raw[e]))
+                jobs.append((encq[e], slice(0, C), stage[:]))
             else:
-                res = terms[j, 0]
-                for e in (2, 1, 3):
-                    res = add_term(j, e, res)
-            nc.sync.dma_start(out=out_rows[j // 2, j % 2], in_=res[:])
+                e = s // 2 + 1
+                interleave_gpsimd(plain_views(stage, dec_raw[e]))
+                jobs.append((decq[e], slice(0, D), stage[:]))
+            if 1 <= s <= 2 * pieces:
+                e, piece = divmod(s - 1, pieces)
+                interleave_w(e, piece)
+                if piece == pieces - 1:
+                    jobs.append((wq[e], slice(0, F), w_stage[e][:]))
+
+            if s == 0:
+                apply_gain(s, 0, 2)
+                tanh(s, (2, 3))
+                empty_third()
+                empty_fourth()
+                apply_gain(s, 2, 4)
+                for k in range(HEAD_PLANES):
+                    widen_next()
+                quantize_x(4, 2)
+                encode(s + 1, (0, 1))
+            elif s == STEPS - 1:
+                decode(s - 1, (0, 1, 2))
+                tanh(s, (0, 1))
+                decode(s - 1, (3,))
+                tanh(s, (2, 3))
+                for i in range(HALF_TILES):
+                    subtract(s - 1, i)
+                    square_sum(s - 1, i)
+                apply_gain(s, 0, 2)
+                apply_gain(s, 2, 4)
+                gate_min(0)
+                gate_exp(0)
+            else:
+                decode(s - 1, (0, 1, 2))
+                if s == 1:
+                    encode(s, (2, 3))
+                tanh(s, (0, 1))
+                decode(s - 1, (3,))
+                subtract(s - 1, 0)
+                subtract(s - 1, 1)
+                apply_gain(s, 0, 2)
+                tanh(s, (2, 3))
+                encode(s + 1, (0, 1))
+                square_sum(s - 1, 0)
+                square_sum(s - 1, 1)
+                subtract(s - 1, 2)
+                apply_gain(s, 2, 4)
+                widen_next()
+                square_sum(s - 1, 2)
+                subtract(s - 1, 3)
+                encode(s + 1, (2, 3))
+                widen_next()
+                square_sum(s - 1, 3)
+            if s == STEPS - 1:
+                project(0, (0, 2))
+            quantize_code(s)
+            if s == 0:
+                quantize_x(6, 2)
+            if s == STEPS - 1:
+                gate_inverse(0)
+                gate_normalise(0)
+            for job in reversed(jobs):
+                quantize(*job)
 
         last = STEPS - 1
-        decode(last)
-        gate_min(0)
-        gate_exp(0)
-        project(0)
-        subtract(last, 0)
-        gate_inverse(0)
-        gate_normalise(0)
-        for i in range(1, HALF_TILES):
-            subtract(last, i)
-        project(1)
+        decode(last, range(HALF_TILES))
+        project(0, (1, 3))
         scalar_terms(0)
+        subtract(last, 0)
+        subtract(last, 1)
         square_sum(last, 0)
         square_sum(last, 1)
+        subtract(last, 2)
+        subtract(last, 3)
+        project(1)
         finish(0)
         project(2)
         scalar_terms(1)
@@ -366,8 +424,15 @@ def tile_expertgateautoencoderrouting_kernel(tc, x, enc, c, dec, w_bytes, w_scal
         gate_inverse(1)
         gate_normalise(1)
         finish(3)
-        for j in range(HALF_TILES, TILES):
-            if j + 1 < TILES:
-                project(j + 1)
+        for j in range(HALF_TILES, TILES - 2):
+            project(j + 1)
             scalar_terms(j)
             finish(j)
+        project(TILES - 1)
+        scalar_terms(TILES - 2)
+        scalar_terms(TILES - 1)
+        steps_a, steps_b = vector_steps(TILES - 2), vector_steps(TILES - 1)
+        while steps_a or steps_b:
+            for steps in (steps_a, steps_b):
+                if steps:
+                    steps.pop(0)()

@@ -60,11 +60,6 @@ def tile_expertgateautoencoderrouting_kernel(tc, x, enc, c, dec, w_bytes, w_scal
                 stop=True,
             )
 
-        c_bf = keep.tile([P, E, PACK], BF16, name="c_bf")
-        nc.scalar.dma_start(out=c_bf[:], in_=c.rearrange("e (p t) -> p e t", t=PACK))
-        ws = keep.tile([P, PACK], F32, name="ws")
-        nc.scalar.dma_start(out=ws[:], in_=w_scale.rearrange("o (p t) z -> p (o t z)", t=PACK))
-
         def load_rows(name, src, dtype):
             raw = keep.tile([P, PACK, 512], dtype, name=name, align_bytes=256)
             nc.sync.dma_start(out=raw[:], in_=src.rearrange("(p j) n -> p j n", j=PACK))
@@ -77,8 +72,13 @@ def tile_expertgateautoencoderrouting_kernel(tc, x, enc, c, dec, w_bytes, w_scal
         for q in range(PAIRS):
             x_sb[q] = keep.tile([P, 2, D], BF16, name="x_sb%d" % q, align_bytes=256)
             nc.sync.dma_start(out=x_sb[q][:], in_=x_rows[q])
+            if q == 0:
+                c_bf = keep.tile([P, E, PACK], BF16, name="c_bf")
+                nc.sync.dma_start(out=c_bf[:], in_=c.rearrange("e (p t) -> p e t", t=PACK))
             if q == DEC_AFTER:
                 dec_raw[0] = load_rows("dec_raw0", dec[0], BF16)
+        ws = keep.tile([P, PACK], F32, name="ws")
+        nc.sync.dma_start(out=ws[:], in_=w_scale.rearrange("o (p t) z -> p (o t z)", t=PACK))
         for e in range(E):
             if e + 1 < E:
                 enc_raw[e + 1] = load_rows("enc_raw%d" % (e + 1), enc[e + 1], BF16)
@@ -98,7 +98,6 @@ def tile_expertgateautoencoderrouting_kernel(tc, x, enc, c, dec, w_bytes, w_scal
         c_f32 = keep.tile([P, E * PACK], F32, name="c_f32")
         nc.scalar.activation(out=c_f32[:], in_=c_bf[:].rearrange("p e t -> p (e t)"), func=ACT.Copy)
         gain = bank([P, E * PACK], "gain")
-        nc.tensor.matmul(gain[:], lhsT=ident[:], rhs=c_f32[:], start=True, stop=True)
 
         def enc_views(stage, raw):
             return (
@@ -190,7 +189,7 @@ def tile_expertgateautoencoderrouting_kernel(tc, x, enc, c, dec, w_bytes, w_scal
 
         def subtract(s, i):
             j = HALF_TILES * (s % 2) + i
-            diffs[s, i] = work.tile([P, D], F32, name="diff", tag="diff", bufs=4)
+            diffs[s, i] = work.tile([P, D], F32, name="diff", tag="diff", bufs=8)
             nc.vector.tensor_tensor(
                 out=diffs[s, i][:], in0=rec_banks[s, i][:], in1=x_sb[j // 2][:, j % 2, :], op=ALU.subtract
             )
@@ -231,6 +230,14 @@ def tile_expertgateautoencoderrouting_kernel(tc, x, enc, c, dec, w_bytes, w_scal
             for i in range(HALF_TILES):
                 nc.scalar.activation(out=gate[h][:, i, :], in_=ez[h][:, i, :], func=ACT.Copy, scale=inv[h][:, i : i + 1])
 
+        gate_psum = {}
+
+        def gate_to_psum(h):
+            gate_psum[h] = bank([P, HALF_TILES * E], "gate_psum")
+            nc.tensor.matmul(
+                gate_psum[h][:], lhsT=ident[:], rhs=gate[h][:].rearrange("p i e -> p (i e)"), start=True, stop=True
+            )
+
         q_banks, terms = {}, {}
 
         def project(j, experts=(0, 2, 1, 3)):
@@ -251,8 +258,9 @@ def tile_expertgateautoencoderrouting_kernel(tc, x, enc, c, dec, w_bytes, w_scal
 
         def add_term(j, e, acc):
             res = work.tile([P, F], F32, name="partial", tag="partial", bufs=10)
+            col = E * (j % HALF_TILES) + e
             nc.vector.scalar_tensor_tensor(
-                out=res[:], in0=q_banks[j, e][:], scalar=g_col(j, e), in1=acc[:], op0=ALU.mult, op1=ALU.add
+                out=res[:], in0=q_banks[j, e][:], scalar=gate_psum[j // HALF_TILES][:, col : col + 1], in1=acc[:], op0=ALU.mult, op1=ALU.add
             )
             return res
 
@@ -290,6 +298,7 @@ def tile_expertgateautoencoderrouting_kernel(tc, x, enc, c, dec, w_bytes, w_scal
         nc.vector.tensor_copy(out=views[0], in_=views[1])
         turn_x(0, 1, nc.scalar.copy, "x_grouped0")()
         turn_x(1, 1, nc.scalar.copy, "x_grouped1")()
+        nc.tensor.matmul(gain[:], lhsT=ident[:], rhs=c_f32[:], start=True, stop=True)
         quantize(encq[0], slice(0, C), head_enc[:])
         quantize_x(0, 1)
         quantize_x(1, 1)
@@ -353,39 +362,43 @@ def tile_expertgateautoencoderrouting_kernel(tc, x, enc, c, dec, w_bytes, w_scal
                     widen_next()
                 quantize_x(4, 2)
                 encode(s + 1, (0, 1))
-            elif s == STEPS - 1:
+            elif s == 1:
                 decode(s - 1, (0, 1, 2))
+                encode(s, (2, 3))
                 tanh(s, (0, 1))
                 decode(s - 1, (3,))
                 tanh(s, (2, 3))
+                encode(s + 1, (0, 1, 2))
+                for i in range(HALF_TILES):
+                    subtract(s - 1, i)
+                encode(s + 1, (3,))
+                apply_gain(s, 0, 4)
+                tanh(s + 1, range(HALF_TILES))
+                for i in range(HALF_TILES):
+                    square_sum(s - 1, i)
+            elif s == STEPS - 1:
+                decode(s - 1, range(HALF_TILES))
                 for i in range(HALF_TILES):
                     subtract(s - 1, i)
                     square_sum(s - 1, i)
-                apply_gain(s, 0, 2)
-                apply_gain(s, 2, 4)
+                apply_gain(s, 0, 4)
                 gate_min(0)
                 gate_exp(0)
             else:
-                decode(s - 1, (0, 1, 2))
-                if s == 1:
-                    encode(s, (2, 3))
-                tanh(s, (0, 1))
-                decode(s - 1, (3,))
-                subtract(s - 1, 0)
-                subtract(s - 1, 1)
-                apply_gain(s, 0, 2)
-                tanh(s, (2, 3))
                 encode(s + 1, (0, 1))
-                square_sum(s - 1, 0)
-                square_sum(s - 1, 1)
-                subtract(s - 1, 2)
-                apply_gain(s, 2, 4)
+                decode(s - 1, (0,))
+                encode(s + 1, (2,))
+                decode(s - 1, (1,))
+                encode(s + 1, (3,))
+                decode(s - 1, (2,))
+                apply_gain(s, 0, 4)
+                tanh(s + 1, range(HALF_TILES))
+                decode(s - 1, (3,))
                 widen_next()
-                square_sum(s - 1, 2)
-                subtract(s - 1, 3)
-                encode(s + 1, (2, 3))
                 widen_next()
-                square_sum(s - 1, 3)
+                for i in range(HALF_TILES):
+                    subtract(s - 1, i)
+                    square_sum(s - 1, i)
             if s == STEPS - 1:
                 project(0, (0, 2))
             quantize_code(s)
@@ -399,38 +412,51 @@ def tile_expertgateautoencoderrouting_kernel(tc, x, enc, c, dec, w_bytes, w_scal
 
         last = STEPS - 1
         decode(last, range(HALF_TILES))
-        project(0, (1, 3))
+        gate_to_psum(0)
         scalar_terms(0)
         subtract(last, 0)
         subtract(last, 1)
+        project(0, (1, 3))
+        project(1, (0, 2))
         square_sum(last, 0)
         square_sum(last, 1)
         subtract(last, 2)
         subtract(last, 3)
-        project(1)
-        finish(0)
-        project(2)
         scalar_terms(1)
+        project(1, (1, 3))
+        project(2, (0, 2))
+        finish(0)
         square_sum(last, 2)
         square_sum(last, 3)
+        project(2, (1, 3))
         finish(1)
-        project(3)
+        project(3, (0, 2))
         scalar_terms(2)
         gate_min(1)
         gate_exp(1)
+        project(3, (1, 3))
         finish(2)
-        project(4)
+        project(4, (0, 2))
         scalar_terms(3)
         gate_inverse(1)
         gate_normalise(1)
+        project(4, (1, 3))
+        gate_to_psum(1)
         finish(3)
-        for j in range(HALF_TILES, TILES - 2):
-            project(j + 1)
-            scalar_terms(j)
-            finish(j)
-        project(TILES - 1)
-        scalar_terms(TILES - 2)
-        scalar_terms(TILES - 1)
+        project(5, (0, 2))
+        scalar_terms(4)
+        project(5, (1, 3))
+        finish(4)
+        project(6, (0, 2))
+        scalar_terms(5)
+        project(7, (0,))
+        project(6, (1,))
+        finish(5)
+        project(7, (2,))
+        scalar_terms(6)
+        scalar_terms(7)
+        project(6, (3,))
+        project(7, (1, 3))
         steps_a, steps_b = vector_steps(TILES - 2), vector_steps(TILES - 1)
         while steps_a or steps_b:
             for steps in (steps_a, steps_b):

@@ -159,10 +159,12 @@ def tile_expertgateautoencoderrouting_kernel(tc, x, enc, c, dec, w_bytes, w_scal
 
         def tanh(s, tiles):
             if s not in tanh_sb:
-                tanh_sb[s] = work.tile([P, HALF_TILES, P, PACK], F32, name="tanh_sb", tag="tanh_sb", bufs=2)
+                tanh_sb[s] = work.tile([P, 2, HALF_TILES * P, 2], F32, name="tanh_sb", tag="tanh_sb", bufs=2)
             for i in tiles:
                 nc.scalar.activation(
-                    out=tanh_sb[s][:, i, :, :], in_=p_banks[s, i][:].rearrange("p t r -> p r t"), func=ACT.Tanh
+                    out=tanh_sb[s][:, :, P * i : P * (i + 1), :],
+                    in_=p_banks[s, i][:].rearrange("p (u v) r -> p u r v", v=2),
+                    func=ACT.Tanh,
                 )
 
         def apply_gain(s, first, last):
@@ -170,9 +172,12 @@ def tile_expertgateautoencoderrouting_kernel(tc, x, enc, c, dec, w_bytes, w_scal
             if first == 0:
                 code_bf[s] = work.tile([P, HALF_TILES * P, PACK], BF16, name="code_bf", tag="code_bf", bufs=2, align_bytes=64)
             nc.vector.tensor_tensor(
-                out=code_bf[s][:, P * first : P * last, :],
-                in0=tanh_sb[s][:, first:last, :, :].rearrange("p n r t -> p (n r) t"),
-                in1=gain[:, PACK * e : PACK * (e + 1)].unsqueeze(1).to_broadcast([P, P * (last - first), PACK]),
+                out=code_bf[s][:, P * first : P * last, :].rearrange("p r (u v) -> p r u v", v=2),
+                in0=tanh_sb[s][:, :, P * first : P * last, :].rearrange("p u r v -> p r u v"),
+                in1=gain[:, PACK * e : PACK * (e + 1)]
+                .rearrange("p (u v) -> p u v", v=2)
+                .unsqueeze(1)
+                .to_broadcast([P, P * (last - first), 2, 2]),
                 op=ALU.mult,
             )
 
@@ -230,14 +235,6 @@ def tile_expertgateautoencoderrouting_kernel(tc, x, enc, c, dec, w_bytes, w_scal
             for i in range(HALF_TILES):
                 nc.scalar.activation(out=gate[h][:, i, :], in_=ez[h][:, i, :], func=ACT.Copy, scale=inv[h][:, i : i + 1])
 
-        gate_psum = {}
-
-        def gate_to_psum(h):
-            gate_psum[h] = bank([P, HALF_TILES * E], "gate_psum")
-            nc.tensor.matmul(
-                gate_psum[h][:], lhsT=ident[:], rhs=gate[h][:].rearrange("p i e -> p (i e)"), start=True, stop=True
-            )
-
         q_banks, terms = {}, {}
 
         def project(j, experts=(0, 2, 1, 3)):
@@ -251,16 +248,15 @@ def tile_expertgateautoencoderrouting_kernel(tc, x, enc, c, dec, w_bytes, w_scal
         def scalar_experts(j):
             return (0,) if j in VECTOR_ONLY else (0, 2)
 
-        def scalar_terms(j):
-            for e in scalar_experts(j):
-                terms[j, e] = work.tile([P, F], F32, name="term", tag="term", bufs=6)
+        def scalar_terms(j, which=slice(0, 2)):
+            for e in scalar_experts(j)[which]:
+                terms[j, e] = work.tile([P, F], F32, name="term", tag="term", bufs=8)
                 nc.scalar.activation(out=terms[j, e][:], in_=q_banks[j, e][:], func=ACT.Copy, scale=g_col(j, e))
 
         def add_term(j, e, acc):
             res = work.tile([P, F], F32, name="partial", tag="partial", bufs=10)
-            col = E * (j % HALF_TILES) + e
             nc.vector.scalar_tensor_tensor(
-                out=res[:], in0=q_banks[j, e][:], scalar=gate_psum[j // HALF_TILES][:, col : col + 1], in1=acc[:], op0=ALU.mult, op1=ALU.add
+                out=res[:], in0=q_banks[j, e][:], scalar=g_col(j, e), in1=acc[:], op0=ALU.mult, op1=ALU.add
             )
             return res
 
@@ -271,7 +267,7 @@ def tile_expertgateautoencoderrouting_kernel(tc, x, enc, c, dec, w_bytes, w_scal
                 def step():
                     sums[j, e] = add_term(j, e, terms[j, e - 1])
                     if e == 3:
-                        res = work.tile([P, F], F32, name="result", tag="result", bufs=3)
+                        res = work.tile([P, F], F32, name="result", tag="result", bufs=6)
                         nc.gpsimd.tensor_tensor(out=res[:], in0=sums[j, 1][:], in1=sums[j, 3][:], op=ALU.add)
                         nc.sync.dma_start(out=out_rows[j // 2, j % 2], in_=res[:])
 
@@ -305,8 +301,10 @@ def tile_expertgateautoencoderrouting_kernel(tc, x, enc, c, dec, w_bytes, w_scal
         turn_x(2, 2, nc.scalar.copy, "x_grouped2")()
         encode(0, (0, 1))
         head_dec = stage_tile("stage_first", 2048)
-        views = plain_views(head_dec, dec_raw[0])
-        nc.vector.tensor_copy(out=views[0], in_=views[1])
+        nc.vector.tensor_copy(
+            out=head_dec[:].rearrange("p (n i j) -> p n j i", i=4, j=PACK),
+            in_=dec_raw[0][:].rearrange("p j (n i) -> p n j i", i=4),
+        )
         tanh(0, (0, 1))
         quantize_x(2, 2)
         quantize(decq[0], slice(0, D), head_dec[:])
@@ -381,9 +379,17 @@ def tile_expertgateautoencoderrouting_kernel(tc, x, enc, c, dec, w_bytes, w_scal
                 for i in range(HALF_TILES):
                     subtract(s - 1, i)
                     square_sum(s - 1, i)
-                apply_gain(s, 0, 4)
+                project(0, (0, 2))
+                project(1, (0, 2))
+                apply_gain(s, 0, 2)
                 gate_min(0)
                 gate_exp(0)
+                apply_gain(s, 2, 3)
+                gate_inverse(0)
+                gate_normalise(0)
+                apply_gain(s, 3, 4)
+                scalar_terms(0)
+                scalar_terms(1)
             else:
                 encode(s + 1, (0, 1))
                 decode(s - 1, (0,))
@@ -400,63 +406,52 @@ def tile_expertgateautoencoderrouting_kernel(tc, x, enc, c, dec, w_bytes, w_scal
                     subtract(s - 1, i)
                     square_sum(s - 1, i)
             if s == STEPS - 1:
-                project(0, (0, 2))
+                quantize(*jobs.pop())
             quantize_code(s)
             if s == 0:
                 quantize_x(6, 2)
-            if s == STEPS - 1:
-                gate_inverse(0)
-                gate_normalise(0)
             for job in reversed(jobs):
                 quantize(*job)
 
         last = STEPS - 1
-        decode(last, range(HALF_TILES))
-        gate_to_psum(0)
-        scalar_terms(0)
-        subtract(last, 0)
-        subtract(last, 1)
         project(0, (1, 3))
-        project(1, (0, 2))
-        square_sum(last, 0)
-        square_sum(last, 1)
-        subtract(last, 2)
-        subtract(last, 3)
-        scalar_terms(1)
-        project(1, (1, 3))
+        decode(last, (0, 1))
         project(2, (0, 2))
+        decode(last, (2, 3))
         finish(0)
-        square_sum(last, 2)
-        square_sum(last, 3)
-        project(2, (1, 3))
-        finish(1)
-        project(3, (0, 2))
+        project(1, (1, 3))
         scalar_terms(2)
+        project(3, (0, 2))
+        for i in range(HALF_TILES):
+            subtract(last, i)
+            square_sum(last, i)
+        project(2, (1, 3))
+        project(3, (1, 3))
+        finish(1)
+        project(4, (0, 2))
+        scalar_terms(3, slice(0, 1))
         gate_min(1)
         gate_exp(1)
-        project(3, (1, 3))
+        scalar_terms(3, slice(1, 2))
+        project(4, (1, 3))
         finish(2)
-        project(4, (0, 2))
-        scalar_terms(3)
         gate_inverse(1)
         gate_normalise(1)
-        project(4, (1, 3))
-        gate_to_psum(1)
-        finish(3)
         project(5, (0, 2))
-        scalar_terms(4)
+        finish(3)
         project(5, (1, 3))
-        finish(4)
+        scalar_terms(4)
         project(6, (0, 2))
-        scalar_terms(5)
+        finish(4)
         project(7, (0,))
         project(6, (1,))
-        finish(5)
+        scalar_terms(5)
         project(7, (2,))
+        project(6, (3,))
+        finish(5)
+        project(7, (1, 3))
         scalar_terms(6)
         scalar_terms(7)
-        project(6, (3,))
-        project(7, (1, 3))
         steps_a, steps_b = vector_steps(TILES - 2), vector_steps(TILES - 1)
         while steps_a or steps_b:
             for steps in (steps_a, steps_b):

@@ -23,7 +23,7 @@ TILES = T // P
 PAIRS = TILES // 2
 HALF_TILES = TILES // 2
 STEPS = 2 * E
-W_CUTS = (0, 176, 344, F)
+W_CUTS = ((0, 192, 320, F), (0, 128, 320, F))
 DEC_AFTER = 1
 HEAD_PLANES = 6
 VECTOR_ONLY = (6, 7)
@@ -101,8 +101,8 @@ def tile_expertgateautoencoderrouting_kernel(tc, x, enc, c, dec, w_bytes, w_scal
 
         def enc_views(stage, raw):
             return (
-                stage[:].rearrange("p (t m j) -> p t m j", t=PACK, j=PACK),
-                raw[:].rearrange("p j (m t) -> p t m j", t=PACK),
+                stage[:].rearrange("p (t m j) -> p m t j", t=PACK, j=PACK),
+                raw[:].rearrange("p j (m t) -> p m t j", t=PACK),
             )
 
         def plain_views(stage, raw):
@@ -290,8 +290,10 @@ def tile_expertgateautoencoderrouting_kernel(tc, x, enc, c, dec, w_bytes, w_scal
                 step()
 
         head_enc = stage_tile("head_enc", 2048)
-        views = enc_views(head_enc, enc_raw[0])
-        nc.vector.tensor_copy(out=views[0], in_=views[1])
+        nc.vector.tensor_copy(
+            out=head_enc[:].rearrange("p (t m i j) -> p m t i j", t=PACK, i=2, j=PACK),
+            in_=enc_raw[0][:].rearrange("p j (m i t) -> p m t i j", t=PACK, i=2),
+        )
         turn_x(0, 1, nc.scalar.copy, "x_grouped0")()
         turn_x(1, 1, nc.scalar.copy, "x_grouped1")()
         nc.tensor.matmul(gain[:], lhsT=ident[:], rhs=c_f32[:], start=True, stop=True)
@@ -317,7 +319,7 @@ def tile_expertgateautoencoderrouting_kernel(tc, x, enc, c, dec, w_bytes, w_scal
         def interleave_w(e, piece):
             if piece == 0:
                 w_stage[e] = stage_tile("stage_second", PACK * F)
-            cols = slice(W_CUTS[piece], W_CUTS[piece + 1])
+            cols = slice(W_CUTS[e][piece], W_CUTS[e][piece + 1])
             views = plain_views(w_stage[e], planes[e])
             interleave_gpsimd((views[0][:, cols, :], views[1][:, cols, :]))
 
@@ -328,7 +330,7 @@ def tile_expertgateautoencoderrouting_kernel(tc, x, enc, c, dec, w_bytes, w_scal
                 e, t = to_widen.pop(0)
                 widen_w(e, [t])
 
-        pieces = len(W_CUTS) - 1
+        pieces = len(W_CUTS[0]) - 1
         for s in range(STEPS):
             jobs = []
             stage = stage_tile("stage_first", 2048)

import math
from contextlib import ExitStack

import concourse.mybir as mybir
from concourse.masks import make_identity

T, D, C, E, F = 1024, 512, 512, 4, 512
TEMPERATURE = 0.05
FLOPS = 3 * E * 2 * T * D * C

F32 = mybir.dt.float32
BF16 = mybir.dt.bfloat16
U32 = mybir.dt.uint32
U8 = mybir.dt.uint8
FP8 = mybir.dt.float8_e4m3fn
FP8X4 = mybir.dt.float8_e4m3fn_x4
ACT = mybir.ActivationFunctionType
ALU = mybir.AluOpType

P = 128
PACK = 4
TILES = T // P
PAIRS = TILES // 2
HALF_TILES = TILES // 2
STEPS = 2 * E
W_CUTS = ((0, 192, 320, F), (0, 128, 320, F))
DEC_AFTER = 1
HEAD_PLANES = 6
VECTOR_ONLY = (6, 7)
ERR_SCALE = math.sqrt(1.0 / (D * TEMPERATURE))


def tile_expertgateautoencoderrouting_kernel(tc, x, enc, c, dec, w_bytes, w_scale, out):
    nc = tc.nc
    with ExitStack() as ctx:
        keep = ctx.enter_context(tc.tile_pool(name="keep", bufs=1))
        work = ctx.enter_context(tc.tile_pool(name="work", bufs=1))
        psum = ctx.enter_context(tc.psum_pool(name="psum", bufs=8))
        ctx.enter_context(tc.manual_schedule())

        def bank(shape, name):
            return psum.tile(shape, F32, name=name, tag="bank")

        def mx_pair(name, width):
            codes = keep.tile([P, width], U32, name=name + "_codes", align_bytes=64)
            scales = keep.tile([P, width], U8, name=name + "_scales", align_bytes=64)
            return codes, scales

        def quantize(pair, cols, src):
            nc.vector.quantize_mx(out=pair[0][:, cols].bitcast(FP8X4), scales=pair[1][:, cols], in_=src)

        def mx_matmul(dst, lhs, lhs_cols, rhs, rhs_cols):
            nc.tensor.matmul_mx(
                out=dst,
                lhsT=lhs[0][:, lhs_cols].bitcast(FP8X4),
                lhsT_scale=lhs[1][:, lhs_cols],
                rhs=rhs[0][:, rhs_cols].bitcast(FP8X4),
                rhs_scale=rhs[1][:, rhs_cols],
                start=True,
                stop=True,
            )

        def load_rows(name, src, dtype):
            raw = keep.tile([P, PACK, 512], dtype, name=name, align_bytes=256)
            nc.sync.dma_start(out=raw[:], in_=src.rearrange("(p j) n -> p j n", j=PACK))
            return raw

        x_rows = x.rearrange("(q p n) d -> q p n d", p=P, n=2)
        out_rows = out.rearrange("(q p n) f -> q n p f", p=P, n=2)
        enc_raw, dec_raw, w_raw, x_sb = {}, {}, {}, {}
        enc_raw[0] = load_rows("enc_raw0", enc[0], BF16)
        for q in range(PAIRS):
            x_sb[q] = keep.tile([P, 2, D], BF16, name="x_sb%d" % q, align_bytes=256)
            nc.sync.dma_start(out=x_sb[q][:], in_=x_rows[q])
            if q == 0:
                c_bf = keep.tile([P, E, PACK], BF16, name="c_bf")
                nc.sync.dma_start(out=c_bf[:], in_=c.rearrange("e (p t) -> p e t", t=PACK))
            if q == DEC_AFTER:
                dec_raw[0] = load_rows("dec_raw0", dec[0], BF16)
        ws = keep.tile([P, PACK], F32, name="ws")
        nc.sync.dma_start(out=ws[:], in_=w_scale.rearrange("o (p t) z -> p (o t z)", t=PACK))
        for e in range(E):
            if e + 1 < E:
                enc_raw[e + 1] = load_rows("enc_raw%d" % (e + 1), enc[e + 1], BF16)
            w_raw[e] = load_rows("w_raw%d" % e, w_bytes[e], U8)
            if e + 1 < E:
                dec_raw[e + 1] = load_rows("dec_raw%d" % (e + 1), dec[e + 1], BF16)

        ident = keep.tile([P, P], F32, name="ident")
        make_identity(nc, ident[:])

        xq = mx_pair("x", T)
        encq = [mx_pair("enc%d" % e, C) for e in range(E)]
        decq = [mx_pair("dec%d" % e, D) for e in range(E)]
        wq = [mx_pair("w%d" % e, F) for e in range(E)]
        ssq = keep.tile([P, TILES, E], F32, name="ssq")

        c_f32 = keep.tile([P, E * PACK], F32, name="c_f32")
        nc.scalar.activation(out=c_f32[:], in_=c_bf[:].rearrange("p e t -> p (e t)"), func=ACT.Copy)
        gain = bank([P, E * PACK], "gain")

        def enc_views(stage, raw):
            return (
                stage[:].rearrange("p (t m j) -> p m t j", t=PACK, j=PACK),
                raw[:].rearrange("p j (m t) -> p m t j", t=PACK),
            )

        def plain_views(stage, raw):
            return stage[:].rearrange("p (n j) -> p n j", j=PACK), raw[:].rearrange("p j n -> p n j")

        def stage_tile(tag, width):
            return work.tile([P, width], BF16, name=tag, tag=tag, align_bytes=64)

        def interleave_gpsimd(views):
            nc.gpsimd.tensor_scalar(views[0], views[1], 1.0, 0.0, op0=ALU.mult, op1=ALU.add)

        planes = {}

        def widen_w(e, slots):
            if e not in planes:
                planes[e] = work.tile([P, PACK, F], BF16, name="w_planes", tag="w_planes", bufs=4)
            for t in slots:
                nc.scalar.activation(
                    out=planes[e][:, t, :], in_=w_raw[e][:, t, :].bitcast(FP8), func=ACT.Copy, scale=ws[:, t : t + 1]
                )

        x_grouped = {}

        def turn_x(first, count, engine_copy, tag):
            xt = bank([P, count, 2, P], "xt")
            for i in range(count):
                q, n = divmod(first + i, 2)
                words = x_sb[q][:].rearrange("p n d -> p (n d)").bitcast(F32)
                for u in range(2):
                    nc.tensor.transpose(xt[:, i, u, :], words[:, 256 * n + u : 256 * (n + 1) : 2], ident[:])
            x_grouped[first] = stage_tile(tag, count * P * PACK)

            def empty():
                engine_copy(
                    out=x_grouped[first][:].bitcast(F32).rearrange("p (n r u) -> p n r u", n=count, u=2),
                    in_=xt[:].rearrange("p n u r -> p n r u"),
                )

            return empty

        def quantize_x(first, count):
            quantize(xq, slice(P * first, P * (first + count)), x_grouped[first][:])

        p_banks, tanh_sb, code_bf, codeq, rec_banks, diffs = {}, {}, {}, {}, {}, {}

        def encode(s, tiles):
            for i in tiles:
                j = HALF_TILES * (s % 2) + i
                p_banks[s, i] = bank([P, PACK, P], "p_bank")
                for t in range(PACK):
                    mx_matmul(
                        p_banks[s, i][:, t, :], encq[s // 2], slice(P * t, P * (t + 1)), xq, slice(P * j, P * (j + 1))
                    )

        def tanh(s, tiles):
            if s not in tanh_sb:
                tanh_sb[s] = work.tile([P, 2, HALF_TILES * P, 2], F32, name="tanh_sb", tag="tanh_sb", bufs=2)
            for i in tiles:
                nc.scalar.activation(
                    out=tanh_sb[s][:, :, P * i : P * (i + 1), :],
                    in_=p_banks[s, i][:].rearrange("p (u v) r -> p u r v", v=2),
                    func=ACT.Tanh,
                )

        def apply_gain(s, first, last):
            e = s // 2
            if first == 0:
                code_bf[s] = work.tile([P, HALF_TILES * P, PACK], BF16, name="code_bf", tag="code_bf", bufs=2, align_bytes=64)
            nc.vector.tensor_tensor(
                out=code_bf[s][:, P * first : P * last, :].rearrange("p r (u v) -> p r u v", v=2),
                in0=tanh_sb[s][:, :, P * first : P * last, :].rearrange("p u r v -> p r u v"),
                in1=gain[:, PACK * e : PACK * (e + 1)]
                .rearrange("p (u v) -> p u v", v=2)
                .unsqueeze(1)
                .to_broadcast([P, P * (last - first), 2, 2]),
                op=ALU.mult,
            )

        def quantize_code(s):
            codes = work.tile([P, 4 * P], U32, name="code_codes", tag="code_codes", bufs=2, align_bytes=64)
            scales = work.tile([P, 4 * P], U8, name="code_scales", tag="code_scales", bufs=2, align_bytes=64)
            codeq[s] = (codes, scales)
            quantize(codeq[s], slice(0, 4 * P), code_bf[s][:].rearrange("p r t -> p (r t)"))

        def decode(s, tiles):
            for i in tiles:
                rec_banks[s, i] = bank([P, D], "rec_bank")
                mx_matmul(rec_banks[s, i][:], codeq[s], slice(P * i, P * (i + 1)), decq[s // 2], slice(0, D))

        def subtract(s, i):
            j = HALF_TILES * (s % 2) + i
            diffs[s, i] = work.tile([P, D], F32, name="diff", tag="diff", bufs=8)
            nc.vector.tensor_tensor(
                out=diffs[s, i][:], in0=rec_banks[s, i][:], in1=x_sb[j // 2][:, j % 2, :], op=ALU.subtract
            )

        def square_sum(s, i):
            j = HALF_TILES * (s % 2) + i
            e = s // 2
            nc.scalar.activation(
                out=diffs[s, i][:], in_=diffs[s, i][:], func=ACT.Square, scale=ERR_SCALE, accum_out=ssq[:, j, e : e + 1]
            )

        least, ez, total, inv, gate = {}, {}, {}, {}, {}

        def gate_min(h):
            least[h] = keep.tile([P, HALF_TILES], F32, name="least%d" % h)
            tiles = slice(HALF_TILES * h, HALF_TILES * (h + 1))
            nc.vector.tensor_reduce(out=least[h][:], in_=ssq[:, tiles, :], axis=mybir.AxisListType.X, op=ALU.min)

        def gate_exp(h):
            ez[h] = keep.tile([P, HALF_TILES, E], F32, name="ez%d" % h)
            total[h] = keep.tile([P, HALF_TILES], F32, name="total%d" % h)
            for i in range(HALF_TILES):
                nc.scalar.activation(
                    out=ez[h][:, i, :],
                    in_=ssq[:, HALF_TILES * h + i, :],
                    func=ACT.Exp,
                    scale=-1.0,
                    bias=least[h][:, i : i + 1],
                    accum_out=total[h][:, i : i + 1],
                )

        def gate_inverse(h):
            inv[h] = keep.tile([P, HALF_TILES], F32, name="inv%d" % h)
            nc.vector.reciprocal(out=inv[h][:], in_=total[h][:])

        def gate_normalise(h):
            gate[h] = keep.tile([P, HALF_TILES, E], F32, name="gate%d" % h)
            for i in range(HALF_TILES):
                nc.scalar.activation(out=gate[h][:, i, :], in_=ez[h][:, i, :], func=ACT.Copy, scale=inv[h][:, i : i + 1])

        q_banks, terms = {}, {}

        def project(j, experts=(0, 2, 1, 3)):
            for e in experts:
                q_banks[j, e] = bank([P, F], "q_bank")
                mx_matmul(q_banks[j, e][:], xq, slice(P * j, P * (j + 1)), wq[e], slice(0, F))

        def g_col(j, e):
            return gate[j // HALF_TILES][:, j % HALF_TILES, e : e + 1]

        def scalar_experts(j):
            return (0,) if j in VECTOR_ONLY else (0, 2)

        def scalar_terms(j, which=slice(0, 2)):
            for e in scalar_experts(j)[which]:
                terms[j, e] = work.tile([P, F], F32, name="term", tag="term", bufs=8)
                nc.scalar.activation(out=terms[j, e][:], in_=q_banks[j, e][:], func=ACT.Copy, scale=g_col(j, e))

        def add_term(j, e, acc):
            res = work.tile([P, F], F32, name="partial", tag="partial", bufs=10)
            nc.vector.scalar_tensor_tensor(
                out=res[:], in0=q_banks[j, e][:], scalar=g_col(j, e), in1=acc[:], op0=ALU.mult, op1=ALU.add
            )
            return res

        sums = {}

        def vector_steps(j):
            def pair_step(e):
                def step():
                    sums[j, e] = add_term(j, e, terms[j, e - 1])
                    if e == 3:
                        res = work.tile([P, F], F32, name="result", tag="result", bufs=6)
                        nc.gpsimd.tensor_tensor(out=res[:], in0=sums[j, 1][:], in1=sums[j, 3][:], op=ALU.add)
                        nc.sync.dma_start(out=out_rows[j // 2, j % 2], in_=res[:])

                return step

            def chain_step(e, before):
                def step():
                    sums[j, e] = add_term(j, e, terms[j, 0] if before is None else sums[j, before])
                    if e == 3:
                        nc.sync.dma_start(out=out_rows[j // 2, j % 2], in_=sums[j, e][:])

                return step

            if j in VECTOR_ONLY:
                return [chain_step(2, None), chain_step(1, 2), chain_step(3, 1)]
            return [pair_step(1), pair_step(3)]

        def finish(j):
            for step in vector_steps(j):
                step()

        head_enc = stage_tile("head_enc", 2048)
        nc.vector.tensor_copy(
            out=head_enc[:].rearrange("p (t m i j) -> p m t i j", t=PACK, i=2, j=PACK),
            in_=enc_raw[0][:].rearrange("p j (m i t) -> p m t i j", t=PACK, i=2),
        )
        turn_x(0, 1, nc.scalar.copy, "x_grouped0")()
        turn_x(1, 1, nc.scalar.copy, "x_grouped1")()
        nc.tensor.matmul(gain[:], lhsT=ident[:], rhs=c_f32[:], start=True, stop=True)
        quantize(encq[0], slice(0, C), head_enc[:])
        quantize_x(0, 1)
        quantize_x(1, 1)
        turn_x(2, 2, nc.scalar.copy, "x_grouped2")()
        encode(0, (0, 1))
        head_dec = stage_tile("stage_first", 2048)
        nc.vector.tensor_copy(
            out=head_dec[:].rearrange("p (n i j) -> p n j i", i=4, j=PACK),
            in_=dec_raw[0][:].rearrange("p j (n i) -> p n j i", i=4),
        )
        tanh(0, (0, 1))
        quantize_x(2, 2)
        quantize(decq[0], slice(0, D), head_dec[:])
        empty_third = turn_x(4, 2, nc.vector.tensor_copy, "x_grouped4")
        encode(0, (2, 3))
        empty_fourth = turn_x(6, 2, nc.vector.tensor_copy, "x_grouped6")

        w_stage = {}

        def interleave_w(e, piece):
            if piece == 0:
                w_stage[e] = stage_tile("stage_second", PACK * F)
            cols = slice(W_CUTS[e][piece], W_CUTS[e][piece + 1])
            views = plain_views(w_stage[e], planes[e])
            interleave_gpsimd((views[0][:, cols, :], views[1][:, cols, :]))

        to_widen = [(e, t) for e in range(E) for t in range(PACK)]

        def widen_next():
            if to_widen:
                e, t = to_widen.pop(0)
                widen_w(e, [t])

        pieces = len(W_CUTS[0]) - 1
        for s in range(STEPS):
            jobs = []
            stage = stage_tile("stage_first", 2048)
            if s >= STEPS - 2:
                e = s - (STEPS - E)
                interleave_gpsimd(plain_views(stage, planes[e]))
                jobs.append((wq[e], slice(0, F), stage[:]))
            elif s % 2 == 0:
                e = s // 2 + 1
                interleave_gpsimd(enc_views(stage, enc_raw[e]))
                jobs.append((encq[e], slice(0, C), stage[:]))
            else:
                e = s // 2 + 1
                interleave_gpsimd(plain_views(stage, dec_raw[e]))
                jobs.append((decq[e], slice(0, D), stage[:]))
            if 1 <= s <= 2 * pieces:
                e, piece = divmod(s - 1, pieces)
                interleave_w(e, piece)
                if piece == pieces - 1:
                    jobs.append((wq[e], slice(0, F), w_stage[e][:]))

            if s == 0:
                apply_gain(s, 0, 2)
                tanh(s, (2, 3))
                empty_third()
                empty_fourth()
                apply_gain(s, 2, 4)
                for k in range(HEAD_PLANES):
                    widen_next()
                quantize_x(4, 2)
                encode(s + 1, (0, 1))
            elif s == 1:
                decode(s - 1, (0, 1, 2))
                encode(s, (2, 3))
                tanh(s, (0, 1))
                decode(s - 1, (3,))
                tanh(s, (2, 3))
                encode(s + 1, (0, 1, 2))
                for i in range(HALF_TILES):
                    subtract(s - 1, i)
                encode(s + 1, (3,))
                apply_gain(s, 0, 4)
                tanh(s + 1, range(HALF_TILES))
                for i in range(HALF_TILES):
                    square_sum(s - 1, i)
            elif s == STEPS - 1:
                decode(s - 1, range(HALF_TILES))
                for i in range(HALF_TILES):
                    subtract(s - 1, i)
                    square_sum(s - 1, i)
                project(0, (0, 2))
                project(1, (0, 2))
                apply_gain(s, 0, 2)
                gate_min(0)
                gate_exp(0)
                apply_gain(s, 2, 3)
                gate_inverse(0)
                gate_normalise(0)
                apply_gain(s, 3, 4)
                scalar_terms(0)
                scalar_terms(1)
            else:
                encode(s + 1, (0, 1))
                decode(s - 1, (0,))
                encode(s + 1, (2,))
                decode(s - 1, (1,))
                encode(s + 1, (3,))
                decode(s - 1, (2,))
                apply_gain(s, 0, 4)
                tanh(s + 1, range(HALF_TILES))
                decode(s - 1, (3,))
                widen_next()
                widen_next()
                for i in range(HALF_TILES):
                    subtract(s - 1, i)
                    square_sum(s - 1, i)
            if s == STEPS - 1:
                quantize(*jobs.pop())
            quantize_code(s)
            if s == 0:
                quantize_x(6, 2)
            for job in reversed(jobs):
                quantize(*job)

        last = STEPS - 1
        project(0, (1, 3))
        decode(last, (0, 1))
        project(2, (0, 2))
        decode(last, (2, 3))
        finish(0)
        project(1, (1, 3))
        scalar_terms(2)
        project(3, (0, 2))
        for i in range(HALF_TILES):
            subtract(last, i)
            square_sum(last, i)
        project(2, (1, 3))
        project(3, (1, 3))
        finish(1)
        project(4, (0, 2))
        scalar_terms(3, slice(0, 1))
        gate_min(1)
        gate_exp(1)
        scalar_terms(3, slice(1, 2))
        project(4, (1, 3))
        finish(2)
        gate_inverse(1)
        gate_normalise(1)
        project(5, (0, 2))
        finish(3)
        project(5, (1, 3))
        scalar_terms(4)
        project(6, (0, 2))
        finish(4)
        project(7, (0,))
        project(6, (1,))
        scalar_terms(5)
        project(7, (2,))
        project(6, (3,))
        finish(5)
        project(7, (1, 3))
        scalar_terms(6)
        scalar_terms(7)
        steps_a, steps_b = vector_steps(TILES - 2), vector_steps(TILES - 1)
        while steps_a or steps_b:
            for steps in (steps_a, steps_b):
                if steps:
                    steps.pop(0)()
